import numpy as np
import ml_dtypes


def mxq(x, axis, fmt="e4m3"):
    dtype, down = {"e4m3": (ml_dtypes.float8_e4m3fn, 7), "e5m2": (ml_dtypes.float8_e5m2, 14)}[fmt]
    v = np.moveaxis(np.asarray(x, np.float32).astype(ml_dtypes.bfloat16).astype(np.float64), axis, -1)
    blocks = v.reshape(v.shape[:-1] + (-1, 32))
    amax = np.abs(blocks).max(-1, keepdims=True)
    byte = np.maximum(np.where(amax > 0, np.frexp(amax)[1] - 1 + 127, 0) - down, 1)
    scale = np.exp2(byte - 127.0)
    codes = (blocks / scale).astype(np.float32).astype(dtype).astype(np.float64)
    return np.moveaxis((codes * scale).reshape(v.shape), -1, axis)


WIDE = False


def mx_kscale(k):
    if not WIDE:
        return np.ones(k)
    levels = np.array([10, -10, 5, -5, 0])
    if k % 512:
        return np.exp2(np.random.permutation(np.resize(levels, k // 32))).repeat(32)
    a = np.empty((k // 512, 16))
    for p in range(k // 512):
        a[p, :8] = np.random.permutation(np.resize(levels, 8))
        for g in range(8):
            far = levels[np.abs(levels - a[p, g]) >= 10]
            a[p, g + 8] = far[np.random.randint(len(far))]
    return np.exp2(a.ravel()).repeat(32)


def f64(x):
    return np.asarray(x).astype(np.float64)


def striped(idx):
    return np.tile(np.asarray(idx).reshape(-1, 16).T, (8, 1)).astype(np.uint16)


def unstriped(offs):
    return offs[:16].T.reshape(-1).astype(np.int64)


E2M1 = np.array([0.0, 0.5, 1.0, 1.5, 2.0, 3.0, 4.0, 6.0, -0.0, -0.5, -1.0, -1.5, -2.0, -3.0, -4.0, -6.0])


def pack_weight(w, fmt):
    k, n = w.shape
    w = f64(np.asarray(w, np.float32).astype(ml_dtypes.bfloat16)).reshape(k // 32, 32, n)
    amax = np.abs(w).max(1)
    if fmt == "e4m3":
        byte = np.frexp(amax)[1] - 1 + 127 - 7
    else:
        mant, ex = np.frexp(amax / 6.0)
        byte = np.where(mant > 0.5, ex, ex - 1) + 127
    byte = np.clip(np.where(amax > 0, byte, 1), 1, 254)
    scaled = (w * np.exp2(127.0 - byte)[:, None, :]).reshape(k, n).astype(np.float32)
    by_word = np.ascontiguousarray(scaled.reshape(k // 512, 128, 4, n).transpose(0, 1, 3, 2))
    if fmt == "e4m3":
        words = by_word.astype(ml_dtypes.float8_e4m3fn).view(np.uint8)
    else:
        c = by_word.astype(ml_dtypes.float4_e2m1fn).view(np.uint8) & 0xF
        words = (c[..., 0::2] | (c[..., 1::2] << 4)).reshape(k // 512, 128, 2 * n)
    return np.ascontiguousarray(words), np.ascontiguousarray(byte.astype(np.uint8).reshape(k // 512, 16, n))


def unpack_weight(words, scales, fmt):
    g, _, n = scales.shape
    words = np.ascontiguousarray(words).reshape(g, 128, n, -1)
    if fmt == "e4m3":
        vals = words.view(ml_dtypes.float8_e4m3fn).astype(np.float64)
    else:
        nib = np.empty((g, 128, n, 4), np.uint8)
        nib[..., 0::2] = words & 0xF
        nib[..., 1::2] = words >> 4
        vals = E2M1[nib]
    vals = vals * np.repeat(np.exp2(scales.astype(np.float64) - 127.0), 8, axis=1)[..., None]
    return vals.transpose(0, 1, 3, 2).reshape(g * 512, n)


B, N, T, D, DV, NQ = 1, 1024, 2048, 1024, 128, 256


def setup_inputs():
    n = np.random.standard_normal
    idx = np.sort(np.random.permutation(T)[:B * N].reshape(B, N), axis=1).reshape(-1)
    s = mx_kscale(D)[:, None]
    u = np.ones(T)
    u[idx] = mx_kscale(B * N)
    r = np.random.uniform(0.5, 2.0, T)
    k = n((D, T)) / s
    v = n((DV, T)) / (u * r)
    kp = pack_weight(k, "e2m1")
    when = np.zeros(T)
    when[idx] = np.sort(np.random.permutation(2 * N)[:B * N])
    return {
        "qT": (n((B, D, NQ)) * s * (0.80 / np.sqrt(D))).astype(np.float32),
        "k_words": np.ascontiguousarray(kp[0].reshape(D // 1024, 2, 128, T, 2).transpose(0, 2, 3, 1, 4)).reshape(D // 1024, 128, T, 4),
        "k_scales": kp[1],
        "vT": v.astype(np.float32),
        "vs": np.tile(u * r, (128, 1)).astype(np.float32),
        "pos": np.tile(when, (128, 1)).astype(np.float32),
        "slope": np.exp2(-np.random.randint(8, 13, (B, NQ, 1))).astype(np.float32),
        "og": n((B, NQ, DV)).astype(np.float32),
        "offs": striped(idx),
    }


def reference(qT, k_words, k_scales, vT, vs, pos, slope, og, offs):
    idx = unstriped(offs)
    k = unpack_weight(k_words.reshape(D // 1024, 128, T, 2, 2).transpose(0, 3, 1, 2, 4).reshape(D // 512, 128, 2 * T), k_scales, "e2m1")
    v = f64(vT)
    pick = lambda x: x[:, idx].reshape(x.shape[0], B, N).transpose(1, 0, 2)
    q = f64(qT)
    score = mxq(q, 1, "e4m3").transpose(0, 2, 1) @ pick(k)
    score = score + f64(slope) * pick(f64(pos))[:, :1, :]
    m = score.max(-1, keepdims=True)
    p = np.exp(score - m)
    total = p.sum(-1, keepdims=True)
    w = p * pick(f64(vs))[:, :1, :]
    y = mxq(w, 2, "e4m3") @ mxq(pick(v).transpose(0, 2, 1), 1, "e4m3")
    y = y / total
    y = y / (1.0 + np.exp(-f64(og)))
    return y

@@ -1,0 +1,234 @@
+from contextlib import ExitStack
+
+import concourse.mybir as mybir
+from concourse.masks import make_identity
+
+N, T, D, DV, NQ = 1024, 2048, 1024, 128, 256
+FLOPS = 2 * NQ * N * D + 2 * NQ * N * DV
+
+F32 = mybir.dt.float32
+BF16 = mybir.dt.bfloat16
+I32 = mybir.dt.int32
+U32 = mybir.dt.uint32
+U16 = mybir.dt.uint16
+U8 = mybir.dt.uint8
+FP8X4 = mybir.dt.float8_e4m3fn_x4
+FP4X4 = mybir.dt.float4_e2m1fn_x4
+ACT = mybir.ActivationFunctionType
+ALU = mybir.AluOpType
+AX = mybir.AxisListType
+
+P = 128
+PACK = 4
+HALF = 512
+
+
+def tile_attend_soft_alibi_gate_srtq256n1024t2048_kernel(tc, qT, k_words, k_scales, vT, vs, pos, slope, og, offs, out):
+    nc = tc.nc
+    with ExitStack() as ctx:
+        sb = ctx.enter_context(tc.tile_pool(name="sb", bufs=1))
+        ps = ctx.enter_context(tc.psum_pool(name="ps", bufs=1))
+
+        def tile(name, shape, dtype):
+            return sb.tile(shape, dtype, name=name, align_bytes=64)
+
+        def bank(tag, name, shape):
+            return ps.tile(shape, F32, name=name, tag=tag)
+
+        offsets = sb.tile([P, N // 16], U16, name="offsets")
+        nc.sync.dma_start(offsets[:], offs)
+
+        def listed(h):
+            return offsets[:, h * HALF // 16 : (h + 1) * HALF // 16]
+
+        scale_pool = tile("scale_pool", [P, T], U8)
+        nc.sync.dma_start(scale_pool[0:32, :].bitcast(I32), k_scales.rearrange("o f t -> f o t").bitcast(I32))
+        vs_pool = tile("vs_pool", [P, T], F32)
+        nc.sync.dma_start(vs_pool[0:32, :], vs[0:32, :])
+        for rows in (slice(32, 64), slice(64, P)):
+            nc.vector.memset(scale_pool[rows, :].bitcast(I32), 0)
+        for rows in (slice(32, 64), slice(64, P)):
+            nc.vector.memset(vs_pool[rows, :], 0.0)
+        ident = tile("ident", [P, P], F32)
+        make_identity(nc, ident[:])
+        k_sc = tile("k_sc", [P, 2 * N], U8)
+        nc.gpsimd.memset(k_sc[:].bitcast(I32), 0)
+
+        word_pool = tile("word_pool", [P, T], I32)
+        nc.sync.dma_start(word_pool[:], k_words[0].rearrange("p t b -> p (t b)").bitcast(I32))
+        q_raw = [tile("q_raw%d" % g, [P, PACK, NQ], F32) for g in range(2)]
+        for g in range(2):
+            nc.sync.dma_start(q_raw[g][:], qT[0, g * 512 : (g + 1) * 512, :].rearrange("(p t) q -> p t q", t=PACK))
+        v_raw = tile("v_raw", [P, T], F32)
+        nc.sync.dma_start(v_raw[:], vT)
+        pos_pool = tile("pos_pool", [P, T], F32)
+        nc.sync.dma_start(pos_pool[:], pos)
+        slope_sb = tile("slope_sb", [P, 2], F32)
+        with nc.allow_non_contiguous_dma(reason="one slope to a partition and query tile"):
+            nc.gpsimd.dma_start(slope_sb[:], slope[0].rearrange("(j p) o -> p (j o)", p=P))
+        og_sb = tile("og_sb", [P, 2, DV], F32)
+        nc.gpsimd.dma_start(og_sb[:], og[0].rearrange("(j p) e -> p j e", p=P))
+
+        sc_listed = tile("sc_listed", [P, N], U8)
+        nc.vector.tensor_copy(sc_listed[:], scale_pool[:].indirect(offsets[:]))
+        for quad in range(4):
+            nc.sync.dma_start(
+                k_sc[32 * quad : 32 * quad + 4, :].bitcast(I32),
+                sc_listed[8 * quad : 8 * quad + 8, :].bitcast(I32),
+            )
+        vs_row = tile("vs_row", [P, N], F32)
+        nc.vector.tensor_copy(vs_row[:], vs_pool[:].indirect(offsets[:]))
+        k_pairs = tile("k_pairs", [P, N], U32)
+        nc.vector.tensor_copy(k_pairs[:], word_pool[:].bitcast(U32).indirect(offsets[:]))
+        k_codes = tile("k_codes", [P, 2, N], U16)
+        nc.vector.tensor_copy(k_codes[:], k_pairs[:].bitcast(U16).rearrange("p (n o) -> p o n", o=2))
+
+        q_grp = tile("q_grp", [P, 2, NQ, PACK], BF16)
+        for g in range(2):
+            nc.scalar.copy(
+                q_grp[:, g].rearrange("p (c i) t -> p c t i", i=4),
+                q_raw[g][:].rearrange("p t (c i) -> p c t i", i=4),
+            )
+        q_codes = tile("q_codes", [P, 2, NQ], U32)
+        q_sc = tile("q_sc", [P, 2, NQ], U8)
+        nc.vector.quantize_mx(
+            out=q_codes[:].rearrange("p g q -> p (g q)").bitcast(FP8X4),
+            scales=q_sc[:].rearrange("p g q -> p (g q)"),
+            in_=q_grp[:].rearrange("p g q t -> p (g q t)"),
+        )
+
+        scores = {}
+        for j in range(2):
+            for h in range(2):
+                scores[j, h] = bank("b%d" % (2 * j + h), "scores%d%d" % (j, h), [P, HALF])
+                for g in range(2):
+                    nc.tensor.matmul_mx(
+                        out=scores[j, h][:],
+                        lhsT=q_codes[:, g, j * P : (j + 1) * P].bitcast(FP8X4),
+                        lhsT_scale=q_sc[:, g, j * P : (j + 1) * P],
+                        rhs=k_codes[:, g, h * HALF : (h + 1) * HALF].bitcast(FP4X4),
+                        rhs_scale=k_sc[:, g * N + h * HALF : g * N + (h + 1) * HALF],
+                        start=(g == 0),
+                        stop=(g == 1),
+                    )
+
+        vs_col = tile("vs_col", [P, 2, PACK], F32)
+        for u in range(2):
+            turned = bank("b%d" % (4 + u), "vs_turned%d" % u, [P, PACK, P])
+            for t in range(PACK):
+                nc.tensor.transpose(turned[:, t, :], vs_row[:, u * HALF + t : (u + 1) * HALF : PACK], ident[:])
+            nc.scalar.copy(vs_col[:, u, :], turned[:, :, 0])
+
+        gate_t = tile("gate_t", [P, 2, DV], F32)
+        nc.scalar.activation(gate_t[:], og_sb[:], ACT.Tanh, scale=0.5)
+        gate = tile("gate", [P, 2, DV], F32)
+        nc.scalar.activation(gate[:], gate_t[:], ACT.Copy, scale=0.5, bias=0.5)
+
+        v_pool = tile("v_pool", [P, T], BF16)
+        nc.scalar.copy(v_pool[:], v_raw[:])
+        v_listed = tile("v_listed", [P, N], BF16)
+        nc.scalar.activation(v_listed[:], v_pool[:].indirect(offsets[:]), ACT.Copy)
+        v_words = v_listed[:].bitcast(F32)
+        v_turned = bank("b6", "v_turned", [P, 2, 2, P])
+        for u in range(2):
+            for e in range(2):
+                nc.tensor.transpose(v_turned[:, u, e, :], v_words[:, 256 * u + e : 256 * (u + 1) : 2], ident[:])
+        v_grp = tile("v_grp", [P, 2, DV, PACK], BF16)
+        nc.scalar.copy(
+            v_grp[:].rearrange("p u e t -> p (u e t)").bitcast(F32).rearrange("p (u e w) -> p u e w", u=2, w=2),
+            v_turned[:].rearrange("p u w e -> p u e w"),
+        )
+
+        pos_row = [tile("pos_row%d" % h, [P, HALF], F32) for h in range(2)]
+        for h in range(2):
+            nc.vector.tensor_copy(pos_row[h][:], pos_pool[:].indirect(listed(h)))
+        s = [tile("s%d" % j, [P, N], F32) for j in range(2)]
+        neg_max = [tile("neg_max%d" % j, [P, 1], F32) for j in range(2)]
+
+        def add_bias(j, h):
+            nc.vector.scalar_tensor_tensor(
+                s[j][:, h * HALF : (h + 1) * HALF], pos_row[h][:], slope_sb[:, j : j + 1], scores[j, h][:], ALU.mult, ALU.add
+            )
+
+        def row_max(j):
+            nc.vector.tensor_reduce(neg_max[j][:], s[j][:], AX.X, ALU.max, negate=True)
+
+        v_codes = tile("v_codes", [P, 2, DV], U32)
+        v_sc = tile("v_sc", [P, 2, DV], U8)
+
+        add_bias(0, 0)
+        add_bias(0, 1)
+        add_bias(1, 0)
+        row_max(0)
+        add_bias(1, 1)
+        nc.vector.quantize_mx(
+            out=v_codes[:].rearrange("p u e -> p (u e)").bitcast(FP8X4),
+            scales=v_sc[:].rearrange("p u e -> p (u e)"),
+            in_=v_grp[:].rearrange("p u e t -> p (u e t)"),
+        )
+        row_max(1)
+
+        sums = tile("sums", [P, 2, 2], F32)
+        p_turned = {}
+        for j in range(2):
+            for u in range(2):
+                p = tile("p%d%d" % (j, u), [P, PACK, P], F32)
+                nc.scalar.activation(
+                    p[:].rearrange("p t s -> p s t"),
+                    s[j][:, u * HALF : (u + 1) * HALF].rearrange("p (s t) -> p s t", t=PACK),
+                    ACT.Exp,
+                    bias=neg_max[j][:],
+                    accum_out=sums[:, u, j : j + 1],
+                )
+                p_turned[j, u] = bank("b%d" % (2 * j + u), "p_turned%d%d" % (j, u), [P, PACK, P])
+                for t in range(PACK):
+                    nc.tensor.transpose(p_turned[j, u][:, t, :], p[:, t, :], ident[:])
+
+        w_grp, w_codes, w_sc = {}, {}, {}
+
+        def weigh(j, u):
+            w_grp[j, u] = tile("w_grp%d%d" % (j, u), [P, P, PACK], BF16)
+            nc.vector.tensor_tensor(
+                w_grp[j, u][:],
+                p_turned[j, u][:].rearrange("p t q -> p q t"),
+                vs_col[:, u, :].unsqueeze(1).to_broadcast([P, P, PACK]),
+                ALU.mult,
+            )
+
+        def quantise_w(j, u):
+            w_codes[j, u] = tile("w_codes%d%d" % (j, u), [P, P], U32)
+            w_sc[j, u] = tile("w_sc%d%d" % (j, u), [P, P], U8)
+            nc.vector.quantize_mx(
+                out=w_codes[j, u][:].bitcast(FP8X4),
+                scales=w_sc[j, u][:],
+                in_=w_grp[j, u][:].rearrange("p q t -> p (q t)"),
+            )
+
+        total = tile("total", [P, 2], F32)
+        inv_total = tile("inv_total", [P, 2], F32)
+        weigh(0, 0)
+        weigh(0, 1)
+        quantise_w(0, 0)
+        weigh(1, 0)
+        quantise_w(0, 1)
+        nc.vector.tensor_tensor(total[:], sums[:, 0, :], sums[:, 1, :], ALU.add)
+        weigh(1, 1)
+        quantise_w(1, 0)
+        nc.vector.reciprocal(inv_total[:], total[:])
+        quantise_w(1, 1)
+
+        for j in range(2):
+            y = bank("b%d" % (4 + j), "y%d" % j, [P, DV])
+            for u in range(2):
+                nc.tensor.matmul_mx(
+                    out=y[:],
+                    lhsT=w_codes[j, u][:].bitcast(FP8X4),
+                    lhsT_scale=w_sc[j, u][:],
+                    rhs=v_codes[:, u, :].bitcast(FP8X4),
+                    rhs_scale=v_sc[:, u, :],
+                    start=(u == 0),
+                    stop=(u == 1),
+                )
+            res = tile("res%d" % j, [P, DV], F32)
+            nc.vector.scalar_tensor_tensor(res[:], y[:], inv_total[:, j : j + 1], gate[:, j, :], ALU.mult, ALU.mult)
+            nc.sync.dma_start(out[0, j * P : (j + 1) * P, :], res[:])

@@ -46,20 +46,20 @@ def tile_attend_soft_alibi_gate_srtq256n1024t2048_kernel(tc, qT, k_words, k_scal
         vs_pool = tile("vs_pool", [P, T], F32)
         nc.sync.dma_start(vs_pool[0:32, :], vs[0:32, :])
         for rows in (slice(32, 64), slice(64, P)):
-            nc.vector.memset(scale_pool[rows, :].bitcast(I32), 0)
-        for rows in (slice(32, 64), slice(64, P)):
-            nc.vector.memset(vs_pool[rows, :], 0.0)
-        ident = tile("ident", [P, P], F32)
-        make_identity(nc, ident[:])
+            nc.gpsimd.memset(scale_pool[rows, :].bitcast(I32), 0)
+        nc.vector.memset(vs_pool[32:64, :], 0.0)
+        nc.gpsimd.memset(vs_pool[64:P, :], 0.0)
         k_sc = tile("k_sc", [P, 2 * N], U8)
         nc.gpsimd.memset(k_sc[:].bitcast(I32), 0)
+        ident = tile("ident", [P, P], F32)
+        make_identity(nc, ident[:])
 
         word_pool = tile("word_pool", [P, T], I32)
         nc.sync.dma_start(word_pool[:], k_words[0].rearrange("p t b -> p (t b)").bitcast(I32))
         q_raw = [tile("q_raw%d" % g, [P, PACK, NQ], F32) for g in range(2)]
         for g in range(2):
             nc.sync.dma_start(q_raw[g][:], qT[0, g * 512 : (g + 1) * 512, :].rearrange("(p t) q -> p t q", t=PACK))
-        v_raw = tile("v_raw", [P, T], F32)
+        v_raw = sb.tile([P, T], F32, name="v_raw", tag="v_raw", align_bytes=64)
         nc.sync.dma_start(v_raw[:], vT)
         pos_pool = tile("pos_pool", [P, T], F32)
         nc.sync.dma_start(pos_pool[:], pos)
@@ -72,7 +72,7 @@ def tile_attend_soft_alibi_gate_srtq256n1024t2048_kernel(tc, qT, k_words, k_scal
         sc_listed = tile("sc_listed", [P, N], U8)
         nc.vector.tensor_copy(sc_listed[:], scale_pool[:].indirect(offsets[:]))
         for quad in range(4):
-            nc.sync.dma_start(
+            nc.scalar.dma_start(
                 k_sc[32 * quad : 32 * quad + 4, :].bitcast(I32),
                 sc_listed[8 * quad : 8 * quad + 8, :].bitcast(I32),
             )
@@ -112,12 +112,11 @@ def tile_attend_soft_alibi_gate_srtq256n1024t2048_kernel(tc, qT, k_words, k_scal
                         stop=(g == 1),
                     )
 
-        vs_col = tile("vs_col", [P, 2, PACK], F32)
+        vs_turned = bank("b7", "vs_turned", [P, 2 * P])
         for u in range(2):
-            turned = bank("b%d" % (4 + u), "vs_turned%d" % u, [P, PACK, P])
             for t in range(PACK):
-                nc.tensor.transpose(turned[:, t, :], vs_row[:, u * HALF + t : (u + 1) * HALF : PACK], ident[:])
-            nc.scalar.copy(vs_col[:, u, :], turned[:, :, 0])
+                at = 2 * (PACK * u + t)
+                nc.tensor.transpose(vs_turned[:, at : at + P], vs_row[:, u * HALF + t : (u + 1) * HALF : PACK], ident[:])
 
         gate_t = tile("gate_t", [P, 2, DV], F32)
         nc.scalar.activation(gate_t[:], og_sb[:], ACT.Tanh, scale=0.5)
@@ -126,6 +125,8 @@ def tile_attend_soft_alibi_gate_srtq256n1024t2048_kernel(tc, qT, k_words, k_scal
 
         v_pool = tile("v_pool", [P, T], BF16)
         nc.scalar.copy(v_pool[:], v_raw[:])
+        vs_col = sb.tile([P, 2, PACK], F32, name="vs_col", tag="v_raw", align_bytes=64)
+        nc.scalar.copy(vs_col[:].rearrange("p u t -> p (u t)"), vs_turned[:, 0 : 4 * PACK : 2])
         v_listed = tile("v_listed", [P, N], BF16)
         nc.scalar.activation(v_listed[:], v_pool[:].indirect(offsets[:]), ACT.Copy)
         v_words = v_listed[:].bitcast(F32)
@@ -168,7 +169,9 @@ def tile_attend_soft_alibi_gate_srtq256n1024t2048_kernel(tc, qT, k_words, k_scal
         )
         row_max(1)
 
-        sums = tile("sums", [P, 2, 2], F32)
+        sums = [tile("sums%d" % j, [P, 2], F32) for j in range(2)]
+        total = [tile("total%d" % j, [P, 1], F32) for j in range(2)]
+        inv_total = [tile("inv_total%d" % j, [P, 1], F32) for j in range(2)]
         p_turned = {}
         for j in range(2):
             for u in range(2):
@@ -178,57 +181,60 @@ def tile_attend_soft_alibi_gate_srtq256n1024t2048_kernel(tc, qT, k_words, k_scal
                     s[j][:, u * HALF : (u + 1) * HALF].rearrange("p (s t) -> p s t", t=PACK),
                     ACT.Exp,
                     bias=neg_max[j][:],
-                    accum_out=sums[:, u, j : j + 1],
+                    accum_out=sums[j][:, u : u + 1],
                 )
                 p_turned[j, u] = bank("b%d" % (2 * j + u), "p_turned%d%d" % (j, u), [P, PACK, P])
                 for t in range(PACK):
                     nc.tensor.transpose(p_turned[j, u][:, t, :], p[:, t, :], ident[:])
+            nc.scalar.activation(total[j][:], sums[j][:, 0:1], ACT.Identity, bias=sums[j][:, 1:2])
 
-        w_grp, w_codes, w_sc = {}, {}, {}
+        w_grp = [tile("w_grp%d" % j, [P, 2, P, PACK], BF16) for j in range(2)]
+        w_codes = [tile("w_codes%d" % j, [P, 2, P], U32) for j in range(2)]
+        w_sc = [tile("w_sc%d" % j, [P, 2, P], U8) for j in range(2)]
 
         def weigh(j, u):
-            w_grp[j, u] = tile("w_grp%d%d" % (j, u), [P, P, PACK], BF16)
             nc.vector.tensor_tensor(
-                w_grp[j, u][:],
+                w_grp[j][:, u],
                 p_turned[j, u][:].rearrange("p t q -> p q t"),
                 vs_col[:, u, :].unsqueeze(1).to_broadcast([P, P, PACK]),
                 ALU.mult,
             )
 
-        def quantise_w(j, u):
-            w_codes[j, u] = tile("w_codes%d%d" % (j, u), [P, P], U32)
-            w_sc[j, u] = tile("w_sc%d%d" % (j, u), [P, P], U8)
+        def quantise_w(j, passes):
             nc.vector.quantize_mx(
-                out=w_codes[j, u][:].bitcast(FP8X4),
-                scales=w_sc[j, u][:],
-                in_=w_grp[j, u][:].rearrange("p q t -> p (q t)"),
+                out=w_codes[j][:, passes].rearrange("p u q -> p (u q)").bitcast(FP8X4),
+                scales=w_sc[j][:, passes].rearrange("p u q -> p (u q)"),
+                in_=w_grp[j][:, passes].rearrange("p u q t -> p (u q t)"),
             )
 
-        total = tile("total", [P, 2], F32)
-        inv_total = tile("inv_total", [P, 2], F32)
-        weigh(0, 0)
-        weigh(0, 1)
-        quantise_w(0, 0)
-        weigh(1, 0)
-        quantise_w(0, 1)
-        nc.vector.tensor_tensor(total[:], sums[:, 0, :], sums[:, 1, :], ALU.add)
-        weigh(1, 1)
-        quantise_w(1, 0)
-        nc.vector.reciprocal(inv_total[:], total[:])
-        quantise_w(1, 1)
-
-        for j in range(2):
+        def multiply(j):
             y = bank("b%d" % (4 + j), "y%d" % j, [P, DV])
             for u in range(2):
                 nc.tensor.matmul_mx(
                     out=y[:],
-                    lhsT=w_codes[j, u][:].bitcast(FP8X4),
-                    lhsT_scale=w_sc[j, u][:],
+                    lhsT=w_codes[j][:, u, :].bitcast(FP8X4),
+                    lhsT_scale=w_sc[j][:, u, :],
                     rhs=v_codes[:, u, :].bitcast(FP8X4),
                     rhs_scale=v_sc[:, u, :],
                     start=(u == 0),
                     stop=(u == 1),
                 )
+            return y
+
+        def finish(j, y):
             res = tile("res%d" % j, [P, DV], F32)
-            nc.vector.scalar_tensor_tensor(res[:], y[:], inv_total[:, j : j + 1], gate[:, j, :], ALU.mult, ALU.mult)
+            nc.vector.scalar_tensor_tensor(res[:], y[:], inv_total[j][:], gate[:, j, :], ALU.mult, ALU.mult)
             nc.sync.dma_start(out[0, j * P : (j + 1) * P, :], res[:])
+
+        weigh(0, 0)
+        weigh(0, 1)
+        nc.vector.reciprocal(inv_total[0][:], total[0][:])
+        quantise_w(0, slice(0, 2))
+        y0 = multiply(0)
+        weigh(1, 0)
+        finish(0, y0)
+        weigh(1, 1)
+        quantise_w(1, slice(0, 1))
+        nc.vector.reciprocal(inv_total[1][:], total[1][:])
+        quantise_w(1, slice(1, 2))
+        finish(1, multiply(1))

from contextlib import ExitStack

import concourse.mybir as mybir
from concourse.masks import make_identity

N, T, D, DV, NQ = 1024, 2048, 1024, 128, 256
FLOPS = 2 * NQ * N * D + 2 * NQ * N * DV

F32 = mybir.dt.float32
BF16 = mybir.dt.bfloat16
I32 = mybir.dt.int32
U32 = mybir.dt.uint32
U16 = mybir.dt.uint16
U8 = mybir.dt.uint8
FP8X4 = mybir.dt.float8_e4m3fn_x4
FP4X4 = mybir.dt.float4_e2m1fn_x4
ACT = mybir.ActivationFunctionType
ALU = mybir.AluOpType
AX = mybir.AxisListType

P = 128
PACK = 4
HALF = 512


def tile_attend_soft_alibi_gate_srtq256n1024t2048_kernel(tc, qT, k_words, k_scales, vT, vs, pos, slope, og, offs, out):
    nc = tc.nc
    with ExitStack() as ctx:
        sb = ctx.enter_context(tc.tile_pool(name="sb", bufs=1))
        ps = ctx.enter_context(tc.psum_pool(name="ps", bufs=1))

        def tile(name, shape, dtype):
            return sb.tile(shape, dtype, name=name, align_bytes=64)

        def bank(tag, name, shape):
            return ps.tile(shape, F32, name=name, tag=tag)

        offsets = sb.tile([P, N // 16], U16, name="offsets")
        nc.sync.dma_start(offsets[:], offs)

        def listed(h):
            return offsets[:, h * HALF // 16 : (h + 1) * HALF // 16]

        scale_pool = tile("scale_pool", [P, T], U8)
        nc.sync.dma_start(scale_pool[0:32, :].bitcast(I32), k_scales.rearrange("o f t -> f o t").bitcast(I32))
        vs_pool = tile("vs_pool", [P, T], F32)
        nc.sync.dma_start(vs_pool[0:32, :], vs[0:32, :])
        for rows in (slice(32, 64), slice(64, P)):
            nc.gpsimd.memset(scale_pool[rows, :].bitcast(I32), 0)
        nc.vector.memset(vs_pool[32:64, :], 0.0)
        nc.gpsimd.memset(vs_pool[64:P, :], 0.0)
        k_sc = tile("k_sc", [P, 2 * N], U8)
        nc.gpsimd.memset(k_sc[:].bitcast(I32), 0)
        ident = tile("ident", [P, P], F32)
        make_identity(nc, ident[:])

        word_pool = tile("word_pool", [P, T], I32)
        nc.sync.dma_start(word_pool[:], k_words[0].rearrange("p t b -> p (t b)").bitcast(I32))
        q_raw = [tile("q_raw%d" % g, [P, PACK, NQ], F32) for g in range(2)]
        for g in range(2):
            nc.sync.dma_start(q_raw[g][:], qT[0, g * 512 : (g + 1) * 512, :].rearrange("(p t) q -> p t q", t=PACK))
        v_raw = sb.tile([P, T], F32, name="v_raw", tag="v_raw", align_bytes=64)
        nc.sync.dma_start(v_raw[:], vT)
        pos_pool = tile("pos_pool", [P, T], F32)
        nc.sync.dma_start(pos_pool[:], pos)
        slope_sb = tile("slope_sb", [P, 2], F32)
        with nc.allow_non_contiguous_dma(reason="one slope to a partition and query tile"):
            nc.gpsimd.dma_start(slope_sb[:], slope[0].rearrange("(j p) o -> p (j o)", p=P))
        og_sb = tile("og_sb", [P, 2, DV], F32)
        nc.gpsimd.dma_start(og_sb[:], og[0].rearrange("(j p) e -> p j e", p=P))

        sc_listed = tile("sc_listed", [P, N], U8)
        nc.vector.tensor_copy(sc_listed[:], scale_pool[:].indirect(offsets[:]))
        for quad in range(4):
            nc.scalar.dma_start(
                k_sc[32 * quad : 32 * quad + 4, :].bitcast(I32),
                sc_listed[8 * quad : 8 * quad + 8, :].bitcast(I32),
            )
        vs_row = tile("vs_row", [P, N], F32)
        nc.vector.tensor_copy(vs_row[:], vs_pool[:].indirect(offsets[:]))
        k_pairs = tile("k_pairs", [P, N], U32)
        nc.vector.tensor_copy(k_pairs[:], word_pool[:].bitcast(U32).indirect(offsets[:]))
        k_codes = tile("k_codes", [P, 2, N], U16)
        nc.vector.tensor_copy(k_codes[:], k_pairs[:].bitcast(U16).rearrange("p (n o) -> p o n", o=2))

        q_grp = tile("q_grp", [P, 2, NQ, PACK], BF16)
        for g in range(2):
            nc.scalar.copy(
                q_grp[:, g].rearrange("p (c i) t -> p c t i", i=4),
                q_raw[g][:].rearrange("p t (c i) -> p c t i", i=4),
            )
        q_codes = tile("q_codes", [P, 2, NQ], U32)
        q_sc = tile("q_sc", [P, 2, NQ], U8)
        nc.vector.quantize_mx(
            out=q_codes[:].rearrange("p g q -> p (g q)").bitcast(FP8X4),
            scales=q_sc[:].rearrange("p g q -> p (g q)"),
            in_=q_grp[:].rearrange("p g q t -> p (g q t)"),
        )

        scores = {}
        for j in range(2):
            for h in range(2):
                scores[j, h] = bank("b%d" % (2 * j + h), "scores%d%d" % (j, h), [P, HALF])
                for g in range(2):
                    nc.tensor.matmul_mx(
                        out=scores[j, h][:],
                        lhsT=q_codes[:, g, j * P : (j + 1) * P].bitcast(FP8X4),
                        lhsT_scale=q_sc[:, g, j * P : (j + 1) * P],
                        rhs=k_codes[:, g, h * HALF : (h + 1) * HALF].bitcast(FP4X4),
                        rhs_scale=k_sc[:, g * N + h * HALF : g * N + (h + 1) * HALF],
                        start=(g == 0),
                        stop=(g == 1),
                    )

        vs_turned = bank("b7", "vs_turned", [P, 2 * P])
        for u in range(2):
            for t in range(PACK):
                at = 2 * (PACK * u + t)
                nc.tensor.transpose(vs_turned[:, at : at + P], vs_row[:, u * HALF + t : (u + 1) * HALF : PACK], ident[:])

        gate_t = tile("gate_t", [P, 2, DV], F32)
        nc.scalar.activation(gate_t[:], og_sb[:], ACT.Tanh, scale=0.5)
        gate = tile("gate", [P, 2, DV], F32)
        nc.scalar.activation(gate[:], gate_t[:], ACT.Copy, scale=0.5, bias=0.5)

        v_pool = tile("v_pool", [P, T], BF16)
        nc.scalar.copy(v_pool[:], v_raw[:])
        vs_col = sb.tile([P, 2, PACK], F32, name="vs_col", tag="v_raw", align_bytes=64)
        nc.scalar.copy(vs_col[:].rearrange("p u t -> p (u t)"), vs_turned[:, 0 : 4 * PACK : 2])
        v_listed = tile("v_listed", [P, N], BF16)
        nc.scalar.activation(v_listed[:], v_pool[:].indirect(offsets[:]), ACT.Copy)
        v_words = v_listed[:].bitcast(F32)
        v_turned = bank("b6", "v_turned", [P, 2, 2, P])
        for u in range(2):
            for e in range(2):
                nc.tensor.transpose(v_turned[:, u, e, :], v_words[:, 256 * u + e : 256 * (u + 1) : 2], ident[:])
        v_grp = tile("v_grp", [P, 2, DV, PACK], BF16)
        nc.scalar.copy(
            v_grp[:].rearrange("p u e t -> p (u e t)").bitcast(F32).rearrange("p (u e w) -> p u e w", u=2, w=2),
            v_turned[:].rearrange("p u w e -> p u e w"),
        )

        pos_row = [tile("pos_row%d" % h, [P, HALF], F32) for h in range(2)]
        for h in range(2):
            nc.vector.tensor_copy(pos_row[h][:], pos_pool[:].indirect(listed(h)))
        s = [tile("s%d" % j, [P, N], F32) for j in range(2)]
        neg_max = [tile("neg_max%d" % j, [P, 1], F32) for j in range(2)]

        def add_bias(j, h):
            nc.vector.scalar_tensor_tensor(
                s[j][:, h * HALF : (h + 1) * HALF], pos_row[h][:], slope_sb[:, j : j + 1], scores[j, h][:], ALU.mult, ALU.add
            )

        def row_max(j):
            nc.vector.tensor_reduce(neg_max[j][:], s[j][:], AX.X, ALU.max, negate=True)

        v_codes = tile("v_codes", [P, 2, DV], U32)
        v_sc = tile("v_sc", [P, 2, DV], U8)

        add_bias(0, 0)
        add_bias(0, 1)
        add_bias(1, 0)
        row_max(0)
        add_bias(1, 1)
        nc.vector.quantize_mx(
            out=v_codes[:].rearrange("p u e -> p (u e)").bitcast(FP8X4),
            scales=v_sc[:].rearrange("p u e -> p (u e)"),
            in_=v_grp[:].rearrange("p u e t -> p (u e t)"),
        )
        row_max(1)

        sums = [tile("sums%d" % j, [P, 2], F32) for j in range(2)]
        total = [tile("total%d" % j, [P, 1], F32) for j in range(2)]
        inv_total = [tile("inv_total%d" % j, [P, 1], F32) for j in range(2)]
        p_turned = {}
        for j in range(2):
            for u in range(2):
                p = tile("p%d%d" % (j, u), [P, PACK, P], F32)
                nc.scalar.activation(
                    p[:].rearrange("p t s -> p s t"),
                    s[j][:, u * HALF : (u + 1) * HALF].rearrange("p (s t) -> p s t", t=PACK),
                    ACT.Exp,
                    bias=neg_max[j][:],
                    accum_out=sums[j][:, u : u + 1],
                )
                p_turned[j, u] = bank("b%d" % (2 * j + u), "p_turned%d%d" % (j, u), [P, PACK, P])
                for t in range(PACK):
                    nc.tensor.transpose(p_turned[j, u][:, t, :], p[:, t, :], ident[:])
            nc.scalar.activation(total[j][:], sums[j][:, 0:1], ACT.Identity, bias=sums[j][:, 1:2])

        w_grp = [tile("w_grp%d" % j, [P, 2, P, PACK], BF16) for j in range(2)]
        w_codes = [tile("w_codes%d" % j, [P, 2, P], U32) for j in range(2)]
        w_sc = [tile("w_sc%d" % j, [P, 2, P], U8) for j in range(2)]

        def weigh(j, u):
            nc.vector.tensor_tensor(
                w_grp[j][:, u],
                p_turned[j, u][:].rearrange("p t q -> p q t"),
                vs_col[:, u, :].unsqueeze(1).to_broadcast([P, P, PACK]),
                ALU.mult,
            )

        def quantise_w(j, passes):
            nc.vector.quantize_mx(
                out=w_codes[j][:, passes].rearrange("p u q -> p (u q)").bitcast(FP8X4),
                scales=w_sc[j][:, passes].rearrange("p u q -> p (u q)"),
                in_=w_grp[j][:, passes].rearrange("p u q t -> p (u q t)"),
            )

        def multiply(j):
            y = bank("b%d" % (4 + j), "y%d" % j, [P, DV])
            for u in range(2):
                nc.tensor.matmul_mx(
                    out=y[:],
                    lhsT=w_codes[j][:, u, :].bitcast(FP8X4),
                    lhsT_scale=w_sc[j][:, u, :],
                    rhs=v_codes[:, u, :].bitcast(FP8X4),
                    rhs_scale=v_sc[:, u, :],
                    start=(u == 0),
                    stop=(u == 1),
                )
            return y

        def finish(j, y):
            res = tile("res%d" % j, [P, DV], F32)
            nc.vector.scalar_tensor_tensor(res[:], y[:], inv_total[j][:], gate[:, j, :], ALU.mult, ALU.mult)
            nc.sync.dma_start(out[0, j * P : (j + 1) * P, :], res[:])

        weigh(0, 0)
        weigh(0, 1)
        nc.vector.reciprocal(inv_total[0][:], total[0][:])
        quantise_w(0, slice(0, 2))
        y0 = multiply(0)
        weigh(1, 0)
        finish(0, y0)
        weigh(1, 1)
        quantise_w(1, slice(0, 1))
        nc.vector.reciprocal(inv_total[1][:], total[1][:])
        quantise_w(1, slice(1, 2))
        finish(1, multiply(1))
